import numpy as np
import ml_dtypes


def mxq(x, axis, fmt="e4m3"):
    dtype, down = {"e4m3": (ml_dtypes.float8_e4m3fn, 7), "e5m2": (ml_dtypes.float8_e5m2, 14)}[fmt]
    v = np.moveaxis(np.asarray(x, np.float32).astype(ml_dtypes.bfloat16).astype(np.float64), axis, -1)
    blocks = v.reshape(v.shape[:-1] + (-1, 32))
    amax = np.abs(blocks).max(-1, keepdims=True)
    byte = np.maximum(np.where(amax > 0, np.frexp(amax)[1] - 1 + 127, 0) - down, 1)
    scale = np.exp2(byte - 127.0)
    codes = (blocks / scale).astype(np.float32).astype(dtype).astype(np.float64)
    return np.moveaxis((codes * scale).reshape(v.shape), -1, axis)


WIDE = False


def mx_kscale(k):
    if not WIDE:
        return np.ones(k)
    levels = np.array([10, -10, 5, -5, 0])
    if k % 512:
        return np.exp2(np.random.permutation(np.resize(levels, k // 32))).repeat(32)
    a = np.empty((k // 512, 16))
    for p in range(k // 512):
        a[p, :8] = np.random.permutation(np.resize(levels, 8))
        for g in range(8):
            far = levels[np.abs(levels - a[p, g]) >= 10]
            a[p, g + 8] = far[np.random.randint(len(far))]
    return np.exp2(a.ravel()).repeat(32)


def f64(x):
    return np.asarray(x).astype(np.float64)


def striped(idx):
    return np.tile(idx.reshape(-1, 16).T, (8, 1)).astype(np.uint16)


def unstriped(offs):
    return offs[:16].T.reshape(-1).astype(np.int64)


def striped8(idx):
    return np.concatenate([x.reshape(-1, 16).T for x in idx]).astype(np.uint16)


def runs(offs, k):
    lists = np.stack([offs[16 * r : 16 * r + 16].T.reshape(-1) for r in range(8)]).astype(np.int64)
    return lists[np.arange(k) % 512 // 64]


def pack_weight(w):
    k, n = w.shape
    w = f64(np.asarray(w, np.float32).astype(ml_dtypes.bfloat16)).reshape(k // 32, 32, n)
    amax = np.abs(w).max(1)
    byte = np.clip(np.where(amax > 0, np.frexp(amax)[1] - 1 + 127 - 7, 1), 1, 254)
    scaled = (w * np.exp2(127.0 - byte)[:, None, :]).reshape(k, n).astype(np.float32)
    words = np.ascontiguousarray(scaled.reshape(k // 512, 128, 4, n).transpose(0, 1, 3, 2)).astype(ml_dtypes.float8_e4m3fn).view(np.uint8)
    return words, np.ascontiguousarray(byte.astype(np.uint8).reshape(k // 512, 16, n))


def unpack_weight(words, scales):
    g, p, n, _ = words.shape
    vals = np.ascontiguousarray(words).view(ml_dtypes.float8_e4m3fn).astype(np.float64) * np.repeat(np.exp2(scales.astype(np.float64) - 127.0), 8, axis=1)[..., None]
    return vals.transpose(0, 1, 3, 2).reshape(g * 512, n)


E2M1 = np.array([0.0, 0.5, 1.0, 1.5, 2.0, 3.0, 4.0, 6.0, -0.0, -0.5, -1.0, -1.5, -2.0, -3.0, -4.0, -6.0])


def pack_fp4(w):
    k, n = w.shape
    w = f64(np.asarray(w, np.float32).astype(ml_dtypes.bfloat16)).reshape(k // 32, 32, n)
    amax = np.abs(w).max(1)
    mant, ex = np.frexp(amax / 6.0)
    byte = np.clip(np.where(amax > 0, np.where(mant > 0.5, ex, ex - 1) + 127, 1), 1, 254)
    scaled = (w * np.exp2(127.0 - byte)[:, None, :]).reshape(k, n).astype(np.float32)
    c = np.ascontiguousarray(scaled.reshape(k // 512, 128, 4, n).transpose(0, 1, 3, 2)).astype(ml_dtypes.float4_e2m1fn).view(np.uint8) & 0xF
    words = (c[..., 0::2] | (c[..., 1::2] << 4)).reshape(k // 512, 128, 2 * n)
    return np.ascontiguousarray(words), np.ascontiguousarray(byte.astype(np.uint8).reshape(k // 512, 16, n))


def unpack_fp4(words, scales):
    g, _, n = scales.shape
    words = np.ascontiguousarray(words).reshape(g, 128, n, 2)
    nib = np.empty((g, 128, n, 4), np.uint8)
    nib[..., 0::2] = words & 0xF
    nib[..., 1::2] = words >> 4
    vals = E2M1[nib] * np.repeat(np.exp2(scales.astype(np.float64) - 127.0), 8, axis=1)[..., None]
    return vals.transpose(0, 1, 3, 2).reshape(g * 512, n)


def sigmoid(v):
    return 1.0 / (1.0 + np.exp(-np.maximum(v, -700.0)))

def planes(y):
    n, m = y.shape
    v = y.astype(np.float32).astype(ml_dtypes.bfloat16).astype(np.float64).reshape(n // 32, 32, m)
    top = np.abs(v).max(1)
    byte = np.clip(np.where(top > 0, np.frexp(top)[1] - 1 + 127 - 7, 1), 1, 254)
    codes = (v * np.exp2(127.0 - byte)[:, None, :]).reshape(n, m).astype(np.float32).astype(ml_dtypes.float8_e4m3fn).view(np.uint8)
    words = codes.reshape(n // 512, 128, 4, m).transpose(0, 1, 3, 2)
    return np.ascontiguousarray(words), np.ascontiguousarray(byte.astype(np.uint8).reshape(n // 512, 16, m))


K, T, S, H, C = 512, 2048, 512, 512, 512


def setup_inputs():
    n = np.random.standard_normal
    s = mx_kscale(K)[:, None]
    packed_xT = pack_weight(n((K, T)) * s)
    packed_w1 = pack_fp4(n((K, H)) / np.sqrt(K) / s)
    return {
        "x_words": packed_xT[0],
        "x_scales": packed_xT[1],
        "w1_words": packed_w1[0],
        "w1_scales": packed_w1[1],
        "sl": np.random.uniform(1.0, 2.0, (H, 1)).astype(np.float32),
        "th": (0.5 * n((H, 1))).astype(np.float32),
        "gs": (np.random.uniform(0.5, 1.5, (K, 1)) / s).astype(np.float32),
        "offs": striped(np.random.permutation(T)[:S]),
        "n1": striped(np.random.permutation(S)),
        "ca": striped(np.random.permutation(T)[:C]),
        "hc": striped8(np.random.randint(0, T, (8, C))),
        "n2": striped(np.random.permutation(S)),
        "n3": striped(np.random.permutation(S)),
    }


def reference(x_words, x_scales, w1_words, w1_scales, sl, th, gs, offs, n1, ca, hc, n2, n3):
    x_ca = unpack_weight(x_words, x_scales)[:, unstriped(ca)]
    xq = unpack_weight(x_words, x_scales)[:, unstriped(offs)]
    y = unpack_fp4(w1_words, w1_scales).T @ xq
    sg = sigmoid(f64(sl) * (y[:, unstriped(n1)] - f64(th)))
    z = f64(gs) * (y * sg)
    zq = mxq(z, 0, "e4m3")
    a = 0.0625 * (x_ca.T @ zq)
    x_hc = unpack_weight(x_words, x_scales)[np.arange(K)[:, None], runs(hc, K)]
    b = 0.0625 * (x_hc.T @ zq)
    out_0 = a + (sigmoid(b[:, unstriped(n3)] - b)) * (a[:, unstriped(n2)] - a)
    return (out_0,) + planes(out_0)

@@ -1,0 +1,244 @@
+from contextlib import ExitStack
+
+import concourse.mybir as mybir
+
+K, T, S, H, C = 512, 2048, 512, 512, 512
+FLOPS = 2 * K * H * S + 2 * 2 * K * C * S
+
+F32 = mybir.dt.float32
+BF16 = mybir.dt.bfloat16
+I32 = mybir.dt.int32
+U32 = mybir.dt.uint32
+U16 = mybir.dt.uint16
+U8 = mybir.dt.uint8
+FP8X4 = mybir.dt.float8_e4m3fn_x4
+FP4X4 = mybir.dt.float4_e2m1fn_x4
+ALU = mybir.AluOpType
+ACT = mybir.ActivationFunctionType
+
+P = 128
+PACK = 4
+HALF = S // 2
+LIST_ROWS = 16
+SCORE_SCALE = 0.0625
+
+
+def tile_picked_cdhpullbesa_none_po_kernel(
+    tc, x_words, x_scales, w1_words, w1_scales, sl, th, gs, offs, n1, ca, hc, n2, n3, out_0, out_1, out_2
+):
+    nc = tc.nc
+    with ExitStack() as ctx:
+        sb = ctx.enter_context(tc.tile_pool(name="sb", bufs=1))
+        chain = ctx.enter_context(tc.tile_pool(name="chain", bufs=1))
+        ps = ctx.enter_context(tc.psum_pool(name="ps", bufs=1))
+
+        def tile(name, shape, dtype):
+            return sb.tile(shape, dtype, name=name, align_bytes=64)
+
+        def dealt(ap):
+            return ap.rearrange("p (t m) -> p m t", t=PACK)
+
+        def listed(ap):
+            return ap.rearrange("p (m t) -> p m t", t=PACK)
+
+        def cols(h):
+            return slice(h * HALF, (h + 1) * HALF)
+
+        def entries(lst, h):
+            return lst[:, h * HALF // LIST_ROWS : (h + 1) * HALF // LIST_ROWS]
+
+        lists = {}
+        for name in ("offs", "hc", "n1", "ca", "n3", "n2"):
+            lists[name] = tile(name + "_list", [P, S // LIST_ROWS], U16)
+
+        x_w = tile("x_w", [P, T], I32)
+        x_s = tile("x_s", [P, T], U8)
+        w_raw = tile("w_raw", [P, 2 * H], U8)
+        w_s_raw = chain.tile([P, H], U8, name="w_s_raw", align_bytes=64, offset=4 * C - 64)
+        hc_s = tile("hc_s", [P, C], U8)
+        sl_sb = tile("sl_sb", [P, PACK], F32)
+        th_sb = tile("th_sb", [P, PACK], F32)
+        gs_sb = tile("gs_sb", [P, PACK], F32)
+
+        nc.gpsimd.memset(x_s[:].bitcast(I32), 0)
+        nc.gpsimd.memset(w_s_raw[:].bitcast(I32), 0)
+        nc.vector.memset(hc_s[:].bitcast(I32), 0)
+
+        x_rows = x_scales[0].bitcast(I32)
+        x_s32 = x_s[:].bitcast(I32)
+        for e in range(2):
+            nc.scalar.dma_start(out=x_s32[e:P:16, :], in_=x_rows[e:16:2, :])
+        for r in range(2, 4):
+            nc.scalar.dma_start(out=x_s32[r:P:32, :], in_=x_rows[r:16:4, :])
+        nc.sync.dma_start(lists["offs"][:], offs)
+        nc.sync.dma_start(lists["hc"][:], hc)
+        nc.sync.dma_start(out=x_w[:], in_=x_words[0].rearrange("p n r -> p (n r)").bitcast(I32))
+        nc.scalar.dma_start(out=w_raw[:].bitcast(I32), in_=w1_words[0].bitcast(I32))
+        w_rows = w1_scales[0].bitcast(I32)
+        w_s32 = w_s_raw[:].bitcast(I32)
+        for r in range(4):
+            queue = nc.gpsimd if r == 3 else nc.scalar
+            queue.dma_start(out=w_s32[r:P:32, :], in_=w_rows[r:16:4, :])
+        nc.sync.dma_start(lists["n1"][:], n1)
+        nc.sync.dma_start(lists["ca"][:], ca)
+        nc.sync.dma_start(lists["n3"][:], n3)
+        nc.sync.dma_start(lists["n2"][:], n2)
+        for dst, src in ((sl_sb, sl), (th_sb, th), (gs_sb, gs)):
+            nc.gpsimd.dma_start(out=dst[:], in_=src.rearrange("(p t) o -> p (t o)", t=PACK))
+
+        words = x_w[:].bitcast(U32)
+
+        xq_s = tile("xq_s", [P, S], U8)
+        nc.vector.tensor_copy(xq_s[:], x_s[:].indirect(lists["offs"][:]))
+        hc_s_listed = tile("hc_s_listed", [P, C], U8)
+        nc.vector.tensor_copy(hc_s_listed[:], x_s[:].indirect(lists["hc"][:]))
+        xq_w = tile("xq_w", [P, S], U32)
+        nc.vector.tensor_copy(xq_w[:], words.indirect(lists["offs"][:]))
+
+        w_w = tile("w_w", [P, 2 * H], U8)
+        nc.scalar.copy(dealt(w_w[:].bitcast(U16)), listed(w_raw[:].bitcast(U16)))
+        w_s = tile("w_s", [P, H], U8)
+        nc.vector.tensor_copy(dealt(w_s[:]), listed(w_s_raw[:]))
+        bias = tile("bias", [P, PACK], F32)
+        nc.vector.scalar_tensor_tensor(bias[:], sl_sb[:], -1.0, th_sb[:], ALU.mult, ALU.mult)
+
+        y = []
+        for t in range(PACK):
+            acc = ps.tile([P, S], F32, name="y_acc%d" % t, tag="bank%d" % t)
+            nc.tensor.matmul_mx(
+                out=acc[:],
+                lhsT=w_w[:, 2 * P * t : 2 * P * (t + 1)].bitcast(FP4X4),
+                lhsT_scale=w_s[:, P * t : P * (t + 1)],
+                rhs=xq_w[:].bitcast(FP8X4),
+                rhs_scale=xq_s[:],
+                start=True,
+                stop=True,
+            )
+            y.append((acc, tile("y%d" % t, [P, S], F32)))
+
+        hc_s_dealt = tile("hc_s_dealt", [P, C], U8)
+        nc.vector.tensor_copy(dealt(hc_s_dealt[:]), listed(hc_s_listed[:]))
+        for r in range(4):
+            src = 16 * (r // 2) + r % 2
+            nc.sync.dma_start(out=hc_s[:].bitcast(I32)[r:P:32, :], in_=hc_s_dealt[:].bitcast(I32)[src:P:32, :])
+        hc_w_listed = chain.tile([P, C], U32, name="hc_w_listed", align_bytes=64, offset=0)
+        nc.vector.tensor_copy(hc_w_listed[:], words.indirect(lists["hc"][:]))
+        ca_w = chain.tile([P, C], U32, name="ca_w", align_bytes=64, offset=4 * C + H - 128)
+        nc.vector.tensor_copy(dealt(ca_w[:]), words.indirect(lists["ca"][:]))
+        hc_w = tile("hc_w", [P, C], U32)
+        nc.vector.tensor_copy(dealt(hc_w[:]), listed(hc_w_listed[:]))
+        ca_s = chain.tile([P, C], U8, name="ca_s", align_bytes=64, offset=0)
+        nc.vector.tensor_copy(dealt(ca_s[:]), x_s[:].indirect(lists["ca"][:]))
+
+        z_w = tile("z_w", [P, S], U32)
+        z_s = tile("z_s", [P, S], U8)
+
+        def interleave(engine_copy, dst, src):
+            engine_copy(dst.rearrange("p (c i t) -> p c t i", i=4, t=PACK), src.rearrange("p t (c i) -> p c t i", i=4))
+
+        for h in range(2):
+            z_rows = tile("z_rows%d" % h, [P, PACK, HALF], BF16)
+            for t in range(PACK):
+                if h == 0:
+                    nc.scalar.copy(y[t][1][:], y[t][0][:])
+                sg = tile("sg%d_%d" % (t, h), [P, HALF], F32)
+                nc.scalar.activation(
+                    sg[:],
+                    y[t][1][:].indirect(entries(lists["n1"], h)),
+                    ACT.Sigmoid,
+                    bias=bias[:, t : t + 1],
+                    scale=sl_sb[:, t : t + 1],
+                )
+                nc.vector.scalar_tensor_tensor(z_rows[:, t, :], y[t][1][:, cols(h)], gs_sb[:, t : t + 1], sg[:], ALU.mult, ALU.mult)
+            z_in = tile("z_in%d" % h, [P, PACK * HALF], BF16)
+            interleave(nc.vector.tensor_copy, z_in[:], z_rows[:])
+            nc.vector.quantize_mx(out=z_w[:, cols(h)].bitcast(FP8X4), scales=z_s[:, cols(h)], in_=z_in[:])
+
+        def score(acc, lhs_w, lhs_s, t, c):
+            nc.tensor.matmul_mx(
+                out=acc[:, c],
+                lhsT=lhs_w[:, P * t : P * (t + 1)].bitcast(FP8X4),
+                lhsT_scale=lhs_s[:, P * t : P * (t + 1)],
+                rhs=z_w[:, c].bitcast(FP8X4),
+                rhs_scale=z_s[:, c],
+                start=True,
+                stop=True,
+            )
+
+        a, b, a_acc, b_acc = [], [], [], []
+        for t in range(PACK):
+            first = (4 + 2 * t) % 8
+            b_acc.append(ps.tile([P, S], F32, name="b_acc%d" % t, tag="bank%d" % first))
+            a_acc.append(ps.tile([P, S], F32, name="a_acc%d" % t, tag="bank%d" % (first + 1)))
+            b.append(tile("b%d" % t, [P, S], F32))
+            a.append(tile("a%d" % t, [P, S], F32))
+
+        def scores(t, c):
+            score(b_acc[t], hc_w, hc_s, t, c)
+            score(a_acc[t], ca_w, ca_s, t, c)
+
+        def leave_psum(t, c):
+            nc.scalar.activation(b[t][:, c], b_acc[t][:, c], ACT.Copy, scale=SCORE_SCALE)
+            nc.scalar.activation(a[t][:, c], a_acc[t][:, c], ACT.Copy, scale=SCORE_SCALE)
+
+        for h in range(2):
+            for t in range(2):
+                scores(t, cols(h))
+            if h == 0:
+                for t in range(2):
+                    leave_psum(t, cols(h))
+        for t in range(2, PACK):
+            scores(t, slice(0, S))
+
+        out_rows = [tile("out_rows%d" % h, [P, PACK, HALF], F32) for h in range(2)]
+        out_w = tile("out_w", [P, S], U32)
+        out_s = tile("out_s", [P, S], U8)
+        out_view = out_0.rearrange("(p t) c -> p t c", t=PACK)
+        out_words = out_1[0].rearrange("p n r -> p (n r)").bitcast(I32)
+        out_scale_rows = out_2[0].bitcast(I32)
+
+        units = [(t, h) for h in range(2) for t in range(PACK)]
+        gate = {}
+
+        def front(t, h):
+            if h == 0:
+                leave_psum(t, cols(1) if t < 2 else slice(0, S))
+            bg = tile("bg%d_%d" % (t, h), [P, HALF], F32)
+            nc.scalar.activation(bg[:], b[t][:].indirect(entries(lists["n3"], h)), ACT.Copy)
+            db = tile("db%d_%d" % (t, h), [P, HALF], F32)
+            nc.vector.tensor_tensor(db[:], bg[:], b[t][:, cols(h)], ALU.subtract)
+            gate[t, h] = tile("gate%d_%d" % (t, h), [P, HALF], F32)
+            nc.scalar.activation(gate[t, h][:], db[:], ACT.Sigmoid)
+
+        def back(t, h):
+            pulled = tile("pulled%d_%d" % (t, h), [P, HALF], F32)
+            nc.vector.tensor_tensor(pulled[:], a[t][:].indirect(entries(lists["n2"], h)), gate[t, h][:], ALU.mult)
+            kept = tile("kept%d_%d" % (t, h), [P, HALF], F32)
+            nc.vector.scalar_tensor_tensor(kept[:], gate[t, h][:], -1.0, a[t][:, cols(h)], ALU.add, ALU.mult)
+            return pulled, kept
+
+        def finish(t, h, pulled, kept):
+            nc.vector.tensor_tensor(out_rows[h][:, t, :], pulled[:], kept[:], ALU.subtract)
+            nc.sync.dma_start(out=out_view[:, t, cols(h)], in_=out_rows[h][:, t, :])
+
+        def planes(h, engine_copy):
+            rounded = tile("rounded%d" % h, [P, PACK * HALF], BF16)
+            interleave(engine_copy, rounded[:], out_rows[h][:])
+            nc.vector.quantize_mx(out=out_w[:, cols(h)].bitcast(FP8X4), scales=out_s[:, cols(h)], in_=rounded[:])
+            nc.sync.dma_start(out=out_words[:, cols(h)], in_=out_w[:, cols(h)].bitcast(I32))
+            quarter = slice(h * HALF // 4, (h + 1) * HALF // 4)
+            for r in range(4):
+                nc.scalar.dma_start(out=out_scale_rows[r:16:4, quarter], in_=out_s[:].bitcast(I32)[r:P:32, quarter])
+
+        front(*units[0])
+        parts = None
+        for u in range(len(units)):
+            if u + 1 < len(units):
+                front(*units[u + 1])
+            if parts is not None:
+                finish(*units[u - 1], *parts)
+            if u == PACK:
+                planes(0, nc.scalar.copy)
+            parts = back(*units[u])
+        finish(*units[-1], *parts)
+        planes(1, nc.vector.tensor_copy)

@@ -29,11 +29,10 @@ def tile_picked_cdhpullbesa_none_po_kernel(
     nc = tc.nc
     with ExitStack() as ctx:
         sb = ctx.enter_context(tc.tile_pool(name="sb", bufs=1))
-        chain = ctx.enter_context(tc.tile_pool(name="chain", bufs=1))
         ps = ctx.enter_context(tc.psum_pool(name="ps", bufs=1))
 
-        def tile(name, shape, dtype):
-            return sb.tile(shape, dtype, name=name, align_bytes=64)
+        def tile(name, shape, dtype, tag=None):
+            return sb.tile(shape, dtype, name=name, tag=tag or name, align_bytes=64)
 
         def dealt(ap):
             return ap.rearrange("p (t m) -> p m t", t=PACK)
@@ -54,44 +53,40 @@ def tile_picked_cdhpullbesa_none_po_kernel(
         x_w = tile("x_w", [P, T], I32)
         x_s = tile("x_s", [P, T], U8)
         w_raw = tile("w_raw", [P, 2 * H], U8)
-        w_s_raw = chain.tile([P, H], U8, name="w_s_raw", align_bytes=64, offset=4 * C - 64)
+        w_s_raw = tile("w_s_raw", [P, H], U8)
         hc_s = tile("hc_s", [P, C], U8)
         sl_sb = tile("sl_sb", [P, PACK], F32)
         th_sb = tile("th_sb", [P, PACK], F32)
         gs_sb = tile("gs_sb", [P, PACK], F32)
 
-        nc.gpsimd.memset(x_s[:].bitcast(I32), 0)
-        nc.gpsimd.memset(w_s_raw[:].bitcast(I32), 0)
-        nc.vector.memset(hc_s[:].bitcast(I32), 0)
+        nc.vector.memset(x_s[:].bitcast(I32), 0)
+        nc.vector.memset(w_s_raw[:].bitcast(I32), 0)
+        nc.gpsimd.memset(hc_s[:].bitcast(I32), 0)
 
         x_rows = x_scales[0].bitcast(I32)
         x_s32 = x_s[:].bitcast(I32)
+        nc.sync.dma_start(lists["offs"][:], offs)
         for e in range(2):
             nc.scalar.dma_start(out=x_s32[e:P:16, :], in_=x_rows[e:16:2, :])
         for r in range(2, 4):
             nc.scalar.dma_start(out=x_s32[r:P:32, :], in_=x_rows[r:16:4, :])
-        nc.sync.dma_start(lists["offs"][:], offs)
-        nc.sync.dma_start(lists["hc"][:], hc)
+        nc.sync.dma_start(out=w_raw[:].bitcast(I32), in_=w1_words[0].bitcast(I32))
         nc.sync.dma_start(out=x_w[:], in_=x_words[0].rearrange("p n r -> p (n r)").bitcast(I32))
-        nc.scalar.dma_start(out=w_raw[:].bitcast(I32), in_=w1_words[0].bitcast(I32))
         w_rows = w1_scales[0].bitcast(I32)
         w_s32 = w_s_raw[:].bitcast(I32)
         for r in range(4):
-            queue = nc.gpsimd if r == 3 else nc.scalar
-            queue.dma_start(out=w_s32[r:P:32, :], in_=w_rows[r:16:4, :])
+            nc.scalar.dma_start(out=w_s32[r:P:32, :], in_=w_rows[r:16:4, :])
         nc.sync.dma_start(lists["n1"][:], n1)
+        nc.sync.dma_start(lists["hc"][:], hc)
         nc.sync.dma_start(lists["ca"][:], ca)
         nc.sync.dma_start(lists["n3"][:], n3)
         nc.sync.dma_start(lists["n2"][:], n2)
-        for dst, src in ((sl_sb, sl), (th_sb, th), (gs_sb, gs)):
+        for dst, src in ((th_sb, th), (sl_sb, sl), (gs_sb, gs)):
             nc.gpsimd.dma_start(out=dst[:], in_=src.rearrange("(p t) o -> p (t o)", t=PACK))
-
         words = x_w[:].bitcast(U32)
 
         xq_s = tile("xq_s", [P, S], U8)
         nc.vector.tensor_copy(xq_s[:], x_s[:].indirect(lists["offs"][:]))
-        hc_s_listed = tile("hc_s_listed", [P, C], U8)
-        nc.vector.tensor_copy(hc_s_listed[:], x_s[:].indirect(lists["hc"][:]))
         xq_w = tile("xq_w", [P, S], U32)
         nc.vector.tensor_copy(xq_w[:], words.indirect(lists["offs"][:]))
 
@@ -116,20 +111,20 @@ def tile_picked_cdhpullbesa_none_po_kernel(
             )
             y.append((acc, tile("y%d" % t, [P, S], F32)))
 
+        hc_s_listed = tile("hc_s_listed", [P, C], U8, tag="w_s_raw")
+        nc.vector.tensor_copy(hc_s_listed[:], x_s[:].indirect(lists["hc"][:]))
         hc_s_dealt = tile("hc_s_dealt", [P, C], U8)
         nc.vector.tensor_copy(dealt(hc_s_dealt[:]), listed(hc_s_listed[:]))
         for r in range(4):
             src = 16 * (r // 2) + r % 2
             nc.sync.dma_start(out=hc_s[:].bitcast(I32)[r:P:32, :], in_=hc_s_dealt[:].bitcast(I32)[src:P:32, :])
-        hc_w_listed = chain.tile([P, C], U32, name="hc_w_listed", align_bytes=64, offset=0)
+        hc_w_listed = tile("hc_w_listed", [P, C], U32, tag="w_s_raw")
         nc.vector.tensor_copy(hc_w_listed[:], words.indirect(lists["hc"][:]))
-        ca_w = chain.tile([P, C], U32, name="ca_w", align_bytes=64, offset=4 * C + H - 128)
-        nc.vector.tensor_copy(dealt(ca_w[:]), words.indirect(lists["ca"][:]))
         hc_w = tile("hc_w", [P, C], U32)
         nc.vector.tensor_copy(dealt(hc_w[:]), listed(hc_w_listed[:]))
-        ca_s = chain.tile([P, C], U8, name="ca_s", align_bytes=64, offset=0)
-        nc.vector.tensor_copy(dealt(ca_s[:]), x_s[:].indirect(lists["ca"][:]))
 
+        ca_s = tile("ca_s", [P, C], U8, tag="w_s_raw")
+        nc.vector.tensor_copy(dealt(ca_s[:]), x_s[:].indirect(lists["ca"][:]))
         z_w = tile("z_w", [P, S], U32)
         z_s = tile("z_s", [P, S], U8)
 
@@ -137,10 +132,11 @@ def tile_picked_cdhpullbesa_none_po_kernel(
             engine_copy(dst.rearrange("p (c i t) -> p c t i", i=4, t=PACK), src.rearrange("p t (c i) -> p c t i", i=4))
 
         for h in range(2):
-            z_rows = tile("z_rows%d" % h, [P, PACK, HALF], BF16)
+            z_rows = tile("z_rows%d" % h, [P, PACK, HALF], BF16, tag="z_rows")
             for t in range(PACK):
                 if h == 0:
-                    nc.scalar.copy(y[t][1][:], y[t][0][:])
+                    leave = nc.scalar.copy if t + 1 < PACK else nc.vector.tensor_copy
+                    leave(y[t][1][:], y[t][0][:])
                 sg = tile("sg%d_%d" % (t, h), [P, HALF], F32)
                 nc.scalar.activation(
                     sg[:],
@@ -153,6 +149,8 @@ def tile_picked_cdhpullbesa_none_po_kernel(
             z_in = tile("z_in%d" % h, [P, PACK * HALF], BF16)
             interleave(nc.vector.tensor_copy, z_in[:], z_rows[:])
             nc.vector.quantize_mx(out=z_w[:, cols(h)].bitcast(FP8X4), scales=z_s[:, cols(h)], in_=z_in[:])
+        ca_w = tile("ca_w", [P, C], U32, tag="z_in1")
+        nc.vector.tensor_copy(dealt(ca_w[:]), words.indirect(lists["ca"][:]))
 
         def score(acc, lhs_w, lhs_s, t, c):
             nc.tensor.matmul_mx(
@@ -165,30 +163,22 @@ def tile_picked_cdhpullbesa_none_po_kernel(
                 stop=True,
             )
 
-        a, b, a_acc, b_acc = [], [], [], []
+        a_acc, b_acc = [], []
         for t in range(PACK):
-            first = (4 + 2 * t) % 8
-            b_acc.append(ps.tile([P, S], F32, name="b_acc%d" % t, tag="bank%d" % first))
-            a_acc.append(ps.tile([P, S], F32, name="a_acc%d" % t, tag="bank%d" % (first + 1)))
-            b.append(tile("b%d" % t, [P, S], F32))
-            a.append(tile("a%d" % t, [P, S], F32))
+            b_acc.append(ps.tile([P, S], F32, name="b_acc%d" % t, tag="bank%d" % (PACK + t)))
+            a_acc.append(ps.tile([P, S], F32, name="a_acc%d" % t, tag="bank%d" % t))
 
-        def scores(t, c):
-            score(b_acc[t], hc_w, hc_s, t, c)
-            score(a_acc[t], ca_w, ca_s, t, c)
+        def leave_psum(dst, acc, c):
+            nc.scalar.activation(dst[:, c], acc[:, c], ACT.Copy, scale=SCORE_SCALE)
 
-        def leave_psum(t, c):
-            nc.scalar.activation(b[t][:, c], b_acc[t][:, c], ACT.Copy, scale=SCORE_SCALE)
-            nc.scalar.activation(a[t][:, c], a_acc[t][:, c], ACT.Copy, scale=SCORE_SCALE)
-
-        for h in range(2):
-            for t in range(2):
-                scores(t, cols(h))
-            if h == 0:
-                for t in range(2):
-                    leave_psum(t, cols(h))
-        for t in range(2, PACK):
-            scores(t, slice(0, S))
+        a, b = {}, {0: tile("b0", [P, S], F32)}
+        for t in range(PACK):
+            score(b_acc[t], hc_w, hc_s, t, cols(0))
+        leave_psum(b[0], b_acc[0], cols(0))
+        for t in range(PACK):
+            score(b_acc[t], hc_w, hc_s, t, cols(1))
+        for t in range(PACK):
+            score(a_acc[t], ca_w, ca_s, t, slice(0, S))
 
         out_rows = [tile("out_rows%d" % h, [P, PACK, HALF], F32) for h in range(2)]
         out_w = tile("out_w", [P, S], U32)
@@ -197,27 +187,25 @@ def tile_picked_cdhpullbesa_none_po_kernel(
         out_words = out_1[0].rearrange("p n r -> p (n r)").bitcast(I32)
         out_scale_rows = out_2[0].bitcast(I32)
 
-        units = [(t, h) for h in range(2) for t in range(PACK)]
         gate = {}
 
-        def front(t, h):
-            if h == 0:
-                leave_psum(t, cols(1) if t < 2 else slice(0, S))
-            bg = tile("bg%d_%d" % (t, h), [P, HALF], F32)
-            nc.scalar.activation(bg[:], b[t][:].indirect(entries(lists["n3"], h)), ACT.Copy)
-            db = tile("db%d_%d" % (t, h), [P, HALF], F32)
-            nc.vector.tensor_tensor(db[:], bg[:], b[t][:, cols(h)], ALU.subtract)
-            gate[t, h] = tile("gate%d_%d" % (t, h), [P, HALF], F32)
-            nc.scalar.activation(gate[t, h][:], db[:], ACT.Sigmoid)
+        def gates(t):
+            for h in range(2):
+                bg = tile("bg%d_%d" % (t, h), [P, HALF], F32)
+                nc.scalar.activation(bg[:], b[t][:].indirect(entries(lists["n3"], h)), ACT.Copy)
+                db = tile("db%d_%d" % (t, h), [P, HALF], F32)
+                nc.vector.tensor_tensor(db[:], bg[:], b[t][:, cols(h)], ALU.subtract)
+                gate[t, h] = tile("gate%d_%d" % (t, h), [P, HALF], F32)
+                nc.scalar.activation(gate[t, h][:], db[:], ACT.Sigmoid)
+            if t + 1 < PACK:
+                b[t + 1] = tile("b%d" % (t + 1), [P, S], F32, tag="bg%d_0" % t)
+                leave_psum(b[t + 1], b_acc[t + 1], slice(0, S))
 
-        def back(t, h):
+        def mix(t, h):
             pulled = tile("pulled%d_%d" % (t, h), [P, HALF], F32)
             nc.vector.tensor_tensor(pulled[:], a[t][:].indirect(entries(lists["n2"], h)), gate[t, h][:], ALU.mult)
             kept = tile("kept%d_%d" % (t, h), [P, HALF], F32)
             nc.vector.scalar_tensor_tensor(kept[:], gate[t, h][:], -1.0, a[t][:, cols(h)], ALU.add, ALU.mult)
-            return pulled, kept
-
-        def finish(t, h, pulled, kept):
             nc.vector.tensor_tensor(out_rows[h][:, t, :], pulled[:], kept[:], ALU.subtract)
             nc.sync.dma_start(out=out_view[:, t, cols(h)], in_=out_rows[h][:, t, :])
 
@@ -226,19 +214,21 @@ def tile_picked_cdhpullbesa_none_po_kernel(
             interleave(engine_copy, rounded[:], out_rows[h][:])
             nc.vector.quantize_mx(out=out_w[:, cols(h)].bitcast(FP8X4), scales=out_s[:, cols(h)], in_=rounded[:])
             nc.sync.dma_start(out=out_words[:, cols(h)], in_=out_w[:, cols(h)].bitcast(I32))
-            quarter = slice(h * HALF // 4, (h + 1) * HALF // 4)
-            for r in range(4):
-                nc.scalar.dma_start(out=out_scale_rows[r:16:4, quarter], in_=out_s[:].bitcast(I32)[r:P:32, quarter])
 
-        front(*units[0])
-        parts = None
-        for u in range(len(units)):
-            if u + 1 < len(units):
-                front(*units[u + 1])
-            if parts is not None:
-                finish(*units[u - 1], *parts)
-            if u == PACK:
+        leave_psum(b[0], b_acc[0], cols(1))
+        a[0] = tile("a0", [P, S], F32)
+        gates(0)
+        leave_psum(a[0], a_acc[0], slice(0, S))
+        for t in range(PACK):
+            mix(t, 0)
+            if t + 1 < PACK:
+                gates(t + 1)
+                a[t + 1] = tile("a%d" % (t + 1), [P, S], F32, tag="gate%d_0" % t)
+                leave_psum(a[t + 1], a_acc[t + 1], slice(0, S))
+            else:
                 planes(0, nc.scalar.copy)
-            parts = back(*units[u])
-        finish(*units[-1], *parts)
+            mix(t, 1)
         planes(1, nc.vector.tensor_copy)
+        for r in range(4):
+            queue = nc.scalar if r % 2 else nc.sync
+            queue.dma_start(out=out_scale_rows[r:16:4, :], in_=out_s[:].bitcast(I32)[r:P:32, :])

@@ -60,6 +60,8 @@ def tile_picked_cdhpullbesa_none_po_kernel(
         gs_sb = tile("gs_sb", [P, PACK], F32)
 
         nc.vector.memset(x_s[:].bitcast(I32), 0)
+        warm = tile("warm", [P, 2], F32)
+        nc.vector.memset(warm[:, 0:1], 0.0)
         nc.vector.memset(w_s_raw[:].bitcast(I32), 0)
         nc.gpsimd.memset(hc_s[:].bitcast(I32), 0)
 
@@ -72,6 +74,7 @@ def tile_picked_cdhpullbesa_none_po_kernel(
             nc.scalar.dma_start(out=x_s32[r:P:32, :], in_=x_rows[r:16:4, :])
         nc.sync.dma_start(out=w_raw[:].bitcast(I32), in_=w1_words[0].bitcast(I32))
         nc.sync.dma_start(out=x_w[:], in_=x_words[0].rearrange("p n r -> p (n r)").bitcast(I32))
+        nc.scalar.activation(warm[:, 1:2], warm[:, 0:1], ACT.Sigmoid)
         w_rows = w1_scales[0].bitcast(I32)
         w_s32 = w_s_raw[:].bitcast(I32)
         for r in range(4):

@@ -21,6 +21,7 @@ PACK = 4
 HALF = S // 2
 LIST_ROWS = 16
 SCORE_SCALE = 0.0625
+SCALAR_FETCHES = ((3, 0),)
 
 
 def tile_picked_cdhpullbesa_none_po_kernel(
@@ -98,7 +99,9 @@ def tile_picked_cdhpullbesa_none_po_kernel(
         w_s = tile("w_s", [P, H], U8)
         nc.vector.tensor_copy(dealt(w_s[:]), listed(w_s_raw[:]))
         bias = tile("bias", [P, PACK], F32)
-        nc.vector.scalar_tensor_tensor(bias[:], sl_sb[:], -1.0, th_sb[:], ALU.mult, ALU.mult)
+        minus_th = tile("minus_th", [P, PACK], F32)
+        nc.gpsimd.tensor_scalar(minus_th[:], th_sb[:], -1.0, 0.0, ALU.mult, ALU.add)
+        nc.gpsimd.tensor_tensor(bias[:], sl_sb[:], minus_th[:], ALU.mult)
 
         y = []
         for t in range(PACK):
@@ -174,10 +177,11 @@ def tile_picked_cdhpullbesa_none_po_kernel(
         def leave_psum(dst, acc, c):
             nc.scalar.activation(dst[:, c], acc[:, c], ACT.Copy, scale=SCORE_SCALE)
 
-        a, b = {}, {0: tile("b0", [P, S], F32)}
+        a, b = {}, {t: tile("b%d" % t, [P, S], F32) for t in range(2)}
         for t in range(PACK):
             score(b_acc[t], hc_w, hc_s, t, cols(0))
-        leave_psum(b[0], b_acc[0], cols(0))
+        for t in range(2):
+            leave_psum(b[t], b_acc[t], cols(0))
         for t in range(PACK):
             score(b_acc[t], hc_w, hc_s, t, cols(1))
         for t in range(PACK):
@@ -200,16 +204,25 @@ def tile_picked_cdhpullbesa_none_po_kernel(
                 nc.vector.tensor_tensor(db[:], bg[:], b[t][:, cols(h)], ALU.subtract)
                 gate[t, h] = tile("gate%d_%d" % (t, h), [P, HALF], F32)
                 nc.scalar.activation(gate[t, h][:], db[:], ACT.Sigmoid)
-            if t + 1 < PACK:
+            if 0 < t < PACK - 1:
                 b[t + 1] = tile("b%d" % (t + 1), [P, S], F32, tag="bg%d_0" % t)
                 leave_psum(b[t + 1], b_acc[t + 1], slice(0, S))
 
         def mix(t, h):
+            fetched = a[t][:].indirect(entries(lists["n2"], h))
             pulled = tile("pulled%d_%d" % (t, h), [P, HALF], F32)
-            nc.vector.tensor_tensor(pulled[:], a[t][:].indirect(entries(lists["n2"], h)), gate[t, h][:], ALU.mult)
-            kept = tile("kept%d_%d" % (t, h), [P, HALF], F32)
-            nc.vector.scalar_tensor_tensor(kept[:], gate[t, h][:], -1.0, a[t][:, cols(h)], ALU.add, ALU.mult)
-            nc.vector.tensor_tensor(out_rows[h][:, t, :], pulled[:], kept[:], ALU.subtract)
+            if (t, h) not in SCALAR_FETCHES:
+                nc.vector.tensor_tensor(pulled[:], fetched, gate[t, h][:], ALU.mult)
+                kept = tile("kept%d_%d" % (t, h), [P, HALF], F32)
+                nc.vector.scalar_tensor_tensor(kept[:], gate[t, h][:], -1.0, a[t][:, cols(h)], ALU.add, ALU.mult)
+                nc.vector.tensor_tensor(out_rows[h][:, t, :], pulled[:], kept[:], ALU.subtract)
+            else:
+                nc.scalar.activation(pulled[:], fetched, ACT.Copy)
+                da = tile("da%d_%d" % (t, h), [P, HALF], F32)
+                nc.vector.tensor_tensor(da[:], pulled[:], a[t][:, cols(h)], ALU.subtract)
+                step = tile("step%d_%d" % (t, h), [P, HALF], F32)
+                nc.vector.tensor_tensor(step[:], da[:], gate[t, h][:], ALU.mult)
+                nc.vector.tensor_tensor(out_rows[h][:, t, :], step[:], a[t][:, cols(h)], ALU.add)
             nc.sync.dma_start(out=out_view[:, t, cols(h)], in_=out_rows[h][:, t, :])
 
         def planes(h, engine_copy):
@@ -218,10 +231,11 @@ def tile_picked_cdhpullbesa_none_po_kernel(
             nc.vector.quantize_mx(out=out_w[:, cols(h)].bitcast(FP8X4), scales=out_s[:, cols(h)], in_=rounded[:])
             nc.sync.dma_start(out=out_words[:, cols(h)], in_=out_w[:, cols(h)].bitcast(I32))
 
-        leave_psum(b[0], b_acc[0], cols(1))
+        for t in range(2):
+            leave_psum(b[t], b_acc[t], cols(1))
         a[0] = tile("a0", [P, S], F32)
         gates(0)
-        leave_psum(a[0], a_acc[0], slice(0, S))
+        nc.vector.tensor_scalar(a[0][:], a_acc[0][:], SCORE_SCALE, None, ALU.mult)
         for t in range(PACK):
             mix(t, 0)
             if t + 1 < PACK:

from contextlib import ExitStack

import concourse.mybir as mybir

K, T, S, H, C = 512, 2048, 512, 512, 512
FLOPS = 2 * K * H * S + 2 * 2 * K * C * S

F32 = mybir.dt.float32
BF16 = mybir.dt.bfloat16
I32 = mybir.dt.int32
U32 = mybir.dt.uint32
U16 = mybir.dt.uint16
U8 = mybir.dt.uint8
FP8X4 = mybir.dt.float8_e4m3fn_x4
FP4X4 = mybir.dt.float4_e2m1fn_x4
ALU = mybir.AluOpType
ACT = mybir.ActivationFunctionType

P = 128
PACK = 4
HALF = S // 2
LIST_ROWS = 16
SCORE_SCALE = 0.0625
SCALAR_FETCHES = ((3, 0),)


def tile_picked_cdhpullbesa_none_po_kernel(
    tc, x_words, x_scales, w1_words, w1_scales, sl, th, gs, offs, n1, ca, hc, n2, n3, out_0, out_1, out_2
):
    nc = tc.nc
    with ExitStack() as ctx:
        sb = ctx.enter_context(tc.tile_pool(name="sb", bufs=1))
        ps = ctx.enter_context(tc.psum_pool(name="ps", bufs=1))

        def tile(name, shape, dtype, tag=None):
            return sb.tile(shape, dtype, name=name, tag=tag or name, align_bytes=64)

        def dealt(ap):
            return ap.rearrange("p (t m) -> p m t", t=PACK)

        def listed(ap):
            return ap.rearrange("p (m t) -> p m t", t=PACK)

        def cols(h):
            return slice(h * HALF, (h + 1) * HALF)

        def entries(lst, h):
            return lst[:, h * HALF // LIST_ROWS : (h + 1) * HALF // LIST_ROWS]

        lists = {}
        for name in ("offs", "hc", "n1", "ca", "n3", "n2"):
            lists[name] = tile(name + "_list", [P, S // LIST_ROWS], U16)

        x_w = tile("x_w", [P, T], I32)
        x_s = tile("x_s", [P, T], U8)
        w_raw = tile("w_raw", [P, 2 * H], U8)
        w_s_raw = tile("w_s_raw", [P, H], U8)
        hc_s = tile("hc_s", [P, C], U8)
        sl_sb = tile("sl_sb", [P, PACK], F32)
        th_sb = tile("th_sb", [P, PACK], F32)
        gs_sb = tile("gs_sb", [P, PACK], F32)

        nc.vector.memset(x_s[:].bitcast(I32), 0)
        warm = tile("warm", [P, 2], F32)
        nc.vector.memset(warm[:, 0:1], 0.0)
        nc.vector.memset(w_s_raw[:].bitcast(I32), 0)
        nc.gpsimd.memset(hc_s[:].bitcast(I32), 0)

        x_rows = x_scales[0].bitcast(I32)
        x_s32 = x_s[:].bitcast(I32)
        nc.sync.dma_start(lists["offs"][:], offs)
        for e in range(2):
            nc.scalar.dma_start(out=x_s32[e:P:16, :], in_=x_rows[e:16:2, :])
        for r in range(2, 4):
            nc.scalar.dma_start(out=x_s32[r:P:32, :], in_=x_rows[r:16:4, :])
        nc.sync.dma_start(out=w_raw[:].bitcast(I32), in_=w1_words[0].bitcast(I32))
        nc.sync.dma_start(out=x_w[:], in_=x_words[0].rearrange("p n r -> p (n r)").bitcast(I32))
        nc.scalar.activation(warm[:, 1:2], warm[:, 0:1], ACT.Sigmoid)
        w_rows = w1_scales[0].bitcast(I32)
        w_s32 = w_s_raw[:].bitcast(I32)
        for r in range(4):
            nc.scalar.dma_start(out=w_s32[r:P:32, :], in_=w_rows[r:16:4, :])
        nc.sync.dma_start(lists["n1"][:], n1)
        nc.sync.dma_start(lists["hc"][:], hc)
        nc.sync.dma_start(lists["ca"][:], ca)
        nc.sync.dma_start(lists["n3"][:], n3)
        nc.sync.dma_start(lists["n2"][:], n2)
        for dst, src in ((th_sb, th), (sl_sb, sl), (gs_sb, gs)):
            nc.gpsimd.dma_start(out=dst[:], in_=src.rearrange("(p t) o -> p (t o)", t=PACK))
        words = x_w[:].bitcast(U32)

        xq_s = tile("xq_s", [P, S], U8)
        nc.vector.tensor_copy(xq_s[:], x_s[:].indirect(lists["offs"][:]))
        xq_w = tile("xq_w", [P, S], U32)
        nc.vector.tensor_copy(xq_w[:], words.indirect(lists["offs"][:]))

        w_w = tile("w_w", [P, 2 * H], U8)
        nc.scalar.copy(dealt(w_w[:].bitcast(U16)), listed(w_raw[:].bitcast(U16)))
        w_s = tile("w_s", [P, H], U8)
        nc.vector.tensor_copy(dealt(w_s[:]), listed(w_s_raw[:]))
        bias = tile("bias", [P, PACK], F32)
        minus_th = tile("minus_th", [P, PACK], F32)
        nc.gpsimd.tensor_scalar(minus_th[:], th_sb[:], -1.0, 0.0, ALU.mult, ALU.add)
        nc.gpsimd.tensor_tensor(bias[:], sl_sb[:], minus_th[:], ALU.mult)

        y = []
        for t in range(PACK):
            acc = ps.tile([P, S], F32, name="y_acc%d" % t, tag="bank%d" % t)
            nc.tensor.matmul_mx(
                out=acc[:],
                lhsT=w_w[:, 2 * P * t : 2 * P * (t + 1)].bitcast(FP4X4),
                lhsT_scale=w_s[:, P * t : P * (t + 1)],
                rhs=xq_w[:].bitcast(FP8X4),
                rhs_scale=xq_s[:],
                start=True,
                stop=True,
            )
            y.append((acc, tile("y%d" % t, [P, S], F32)))

        hc_s_listed = tile("hc_s_listed", [P, C], U8, tag="w_s_raw")
        nc.vector.tensor_copy(hc_s_listed[:], x_s[:].indirect(lists["hc"][:]))
        hc_s_dealt = tile("hc_s_dealt", [P, C], U8)
        nc.vector.tensor_copy(dealt(hc_s_dealt[:]), listed(hc_s_listed[:]))
        for r in range(4):
            src = 16 * (r // 2) + r % 2
            nc.sync.dma_start(out=hc_s[:].bitcast(I32)[r:P:32, :], in_=hc_s_dealt[:].bitcast(I32)[src:P:32, :])
        hc_w_listed = tile("hc_w_listed", [P, C], U32, tag="w_s_raw")
        nc.vector.tensor_copy(hc_w_listed[:], words.indirect(lists["hc"][:]))
        hc_w = tile("hc_w", [P, C], U32)
        nc.vector.tensor_copy(dealt(hc_w[:]), listed(hc_w_listed[:]))

        ca_s = tile("ca_s", [P, C], U8, tag="w_s_raw")
        nc.vector.tensor_copy(dealt(ca_s[:]), x_s[:].indirect(lists["ca"][:]))
        z_w = tile("z_w", [P, S], U32)
        z_s = tile("z_s", [P, S], U8)

        def interleave(engine_copy, dst, src):
            engine_copy(dst.rearrange("p (c i t) -> p c t i", i=4, t=PACK), src.rearrange("p t (c i) -> p c t i", i=4))

        for h in range(2):
            z_rows = tile("z_rows%d" % h, [P, PACK, HALF], BF16, tag="z_rows")
            for t in range(PACK):
                if h == 0:
                    leave = nc.scalar.copy if t + 1 < PACK else nc.vector.tensor_copy
                    leave(y[t][1][:], y[t][0][:])
                sg = tile("sg%d_%d" % (t, h), [P, HALF], F32)
                nc.scalar.activation(
                    sg[:],
                    y[t][1][:].indirect(entries(lists["n1"], h)),
                    ACT.Sigmoid,
                    bias=bias[:, t : t + 1],
                    scale=sl_sb[:, t : t + 1],
                )
                nc.vector.scalar_tensor_tensor(z_rows[:, t, :], y[t][1][:, cols(h)], gs_sb[:, t : t + 1], sg[:], ALU.mult, ALU.mult)
            z_in = tile("z_in%d" % h, [P, PACK * HALF], BF16)
            interleave(nc.vector.tensor_copy, z_in[:], z_rows[:])
            nc.vector.quantize_mx(out=z_w[:, cols(h)].bitcast(FP8X4), scales=z_s[:, cols(h)], in_=z_in[:])
        ca_w = tile("ca_w", [P, C], U32, tag="z_in1")
        nc.vector.tensor_copy(dealt(ca_w[:]), words.indirect(lists["ca"][:]))

        def score(acc, lhs_w, lhs_s, t, c):
            nc.tensor.matmul_mx(
                out=acc[:, c],
                lhsT=lhs_w[:, P * t : P * (t + 1)].bitcast(FP8X4),
                lhsT_scale=lhs_s[:, P * t : P * (t + 1)],
                rhs=z_w[:, c].bitcast(FP8X4),
                rhs_scale=z_s[:, c],
                start=True,
                stop=True,
            )

        a_acc, b_acc = [], []
        for t in range(PACK):
            b_acc.append(ps.tile([P, S], F32, name="b_acc%d" % t, tag="bank%d" % (PACK + t)))
            a_acc.append(ps.tile([P, S], F32, name="a_acc%d" % t, tag="bank%d" % t))

        def leave_psum(dst, acc, c):
            nc.scalar.activation(dst[:, c], acc[:, c], ACT.Copy, scale=SCORE_SCALE)

        a, b = {}, {t: tile("b%d" % t, [P, S], F32) for t in range(2)}
        for t in range(PACK):
            score(b_acc[t], hc_w, hc_s, t, cols(0))
        for t in range(2):
            leave_psum(b[t], b_acc[t], cols(0))
        for t in range(PACK):
            score(b_acc[t], hc_w, hc_s, t, cols(1))
        for t in range(PACK):
            score(a_acc[t], ca_w, ca_s, t, slice(0, S))

        out_rows = [tile("out_rows%d" % h, [P, PACK, HALF], F32) for h in range(2)]
        out_w = tile("out_w", [P, S], U32)
        out_s = tile("out_s", [P, S], U8)
        out_view = out_0.rearrange("(p t) c -> p t c", t=PACK)
        out_words = out_1[0].rearrange("p n r -> p (n r)").bitcast(I32)
        out_scale_rows = out_2[0].bitcast(I32)

        gate = {}

        def gates(t):
            for h in range(2):
                bg = tile("bg%d_%d" % (t, h), [P, HALF], F32)
                nc.scalar.activation(bg[:], b[t][:].indirect(entries(lists["n3"], h)), ACT.Copy)
                db = tile("db%d_%d" % (t, h), [P, HALF], F32)
                nc.vector.tensor_tensor(db[:], bg[:], b[t][:, cols(h)], ALU.subtract)
                gate[t, h] = tile("gate%d_%d" % (t, h), [P, HALF], F32)
                nc.scalar.activation(gate[t, h][:], db[:], ACT.Sigmoid)
            if 0 < t < PACK - 1:
                b[t + 1] = tile("b%d" % (t + 1), [P, S], F32, tag="bg%d_0" % t)
                leave_psum(b[t + 1], b_acc[t + 1], slice(0, S))

        def mix(t, h):
            fetched = a[t][:].indirect(entries(lists["n2"], h))
            pulled = tile("pulled%d_%d" % (t, h), [P, HALF], F32)
            if (t, h) not in SCALAR_FETCHES:
                nc.vector.tensor_tensor(pulled[:], fetched, gate[t, h][:], ALU.mult)
                kept = tile("kept%d_%d" % (t, h), [P, HALF], F32)
                nc.vector.scalar_tensor_tensor(kept[:], gate[t, h][:], -1.0, a[t][:, cols(h)], ALU.add, ALU.mult)
                nc.vector.tensor_tensor(out_rows[h][:, t, :], pulled[:], kept[:], ALU.subtract)
            else:
                nc.scalar.activation(pulled[:], fetched, ACT.Copy)
                da = tile("da%d_%d" % (t, h), [P, HALF], F32)
                nc.vector.tensor_tensor(da[:], pulled[:], a[t][:, cols(h)], ALU.subtract)
                step = tile("step%d_%d" % (t, h), [P, HALF], F32)
                nc.vector.tensor_tensor(step[:], da[:], gate[t, h][:], ALU.mult)
                nc.vector.tensor_tensor(out_rows[h][:, t, :], step[:], a[t][:, cols(h)], ALU.add)
            nc.sync.dma_start(out=out_view[:, t, cols(h)], in_=out_rows[h][:, t, :])

        def planes(h, engine_copy):
            rounded = tile("rounded%d" % h, [P, PACK * HALF], BF16)
            interleave(engine_copy, rounded[:], out_rows[h][:])
            nc.vector.quantize_mx(out=out_w[:, cols(h)].bitcast(FP8X4), scales=out_s[:, cols(h)], in_=rounded[:])
            nc.sync.dma_start(out=out_words[:, cols(h)], in_=out_w[:, cols(h)].bitcast(I32))

        for t in range(2):
            leave_psum(b[t], b_acc[t], cols(1))
        a[0] = tile("a0", [P, S], F32)
        gates(0)
        nc.vector.tensor_scalar(a[0][:], a_acc[0][:], SCORE_SCALE, None, ALU.mult)
        for t in range(PACK):
            mix(t, 0)
            if t + 1 < PACK:
                gates(t + 1)
                a[t + 1] = tile("a%d" % (t + 1), [P, S], F32, tag="gate%d_0" % t)
                leave_psum(a[t + 1], a_acc[t + 1], slice(0, S))
            else:
                planes(0, nc.scalar.copy)
            mix(t, 1)
        planes(1, nc.vector.tensor_copy)
        for r in range(4):
            queue = nc.scalar if r % 2 else nc.sync
            queue.dma_start(out=out_scale_rows[r:16:4, :], in_=out_s[:].bitcast(I32)[r:P:32, :])
